import numpy as np
import ml_dtypes


def mxq(x, axis, fmt="e4m3"):
    dtype, down = {"e4m3": (ml_dtypes.float8_e4m3fn, 7), "e5m2": (ml_dtypes.float8_e5m2, 14)}[fmt]
    v = np.moveaxis(np.asarray(x, np.float32).astype(ml_dtypes.bfloat16).astype(np.float64), axis, -1)
    blocks = v.reshape(v.shape[:-1] + (-1, 32))
    amax = np.abs(blocks).max(-1, keepdims=True)
    byte = np.maximum(np.where(amax > 0, np.frexp(amax)[1] - 1 + 127, 0) - down, 1)
    scale = np.exp2(byte - 127.0)
    codes = (blocks / scale).astype(np.float32).astype(dtype).astype(np.float64)
    return np.moveaxis((codes * scale).reshape(v.shape), -1, axis)


WIDE = False


def mx_kscale(k):
    if not WIDE:
        return np.ones(k)
    levels = np.array([10, -10, 5, -5, 0])
    if k % 512:
        return np.exp2(np.random.permutation(np.resize(levels, k // 32))).repeat(32)
    a = np.empty((k // 512, 16))
    for p in range(k // 512):
        a[p, :8] = np.random.permutation(np.resize(levels, 8))
        for g in range(8):
            far = levels[np.abs(levels - a[p, g]) >= 10]
            a[p, g + 8] = far[np.random.randint(len(far))]
    return np.exp2(a.ravel()).repeat(32)


def f64(x):
    return np.asarray(x).astype(np.float64)


def striped(idx):
    return np.tile(idx.reshape(-1, 16).T, (8, 1)).astype(np.uint16)


def unstriped(offs):
    return offs[:16].T.reshape(-1).astype(np.int64)


def striped8(idx):
    return np.concatenate([x.reshape(-1, 16).T for x in idx]).astype(np.uint16)


def runs(offs, k):
    lists = np.stack([offs[16 * r : 16 * r + 16].T.reshape(-1) for r in range(8)]).astype(np.int64)
    return lists[np.arange(k) % 512 // 64]


def pack_weight(w):
    k, n = w.shape
    w = f64(np.asarray(w, np.float32).astype(ml_dtypes.bfloat16)).reshape(k // 32, 32, n)
    amax = np.abs(w).max(1)
    byte = np.clip(np.where(amax > 0, np.frexp(amax)[1] - 1 + 127 - 7, 1), 1, 254)
    scaled = (w * np.exp2(127.0 - byte)[:, None, :]).reshape(k, n).astype(np.float32)
    words = np.ascontiguousarray(scaled.reshape(k // 512, 128, 4, n).transpose(0, 1, 3, 2)).astype(ml_dtypes.float8_e4m3fn).view(np.uint8)
    return words, np.ascontiguousarray(byte.astype(np.uint8).reshape(k // 512, 16, n))


def unpack_weight(words, scales):
    g, p, n, _ = words.shape
    vals = np.ascontiguousarray(words).view(ml_dtypes.float8_e4m3fn).astype(np.float64) * np.repeat(np.exp2(scales.astype(np.float64) - 127.0), 8, axis=1)[..., None]
    return vals.transpose(0, 1, 3, 2).reshape(g * 512, n)


K, T, S, G, H, C = 512, 1024, 512, 2048, 512, 512


def setup_inputs():
    n = np.random.standard_normal
    s = mx_kscale(K)[:, None]
    packed_xT = pack_weight(n((K, T)) * s)
    packed_dT = pack_weight(n((K, G)) / s)
    return {
        "x_words": packed_xT[0],
        "x_scales": packed_xT[1],
        "d_words": packed_dT[0],
        "d_scales": packed_dT[1],
        "gs": (np.random.uniform(0.5, 1.5, (K, 1)) / s).astype(np.float32),
        "offs": striped(np.random.permutation(T)[:S]),
        "k1": striped8(np.random.randint(0, G, (8, H))),
        "n1": striped8(np.stack([np.random.permutation(S) for _ in range(8)])),
        "n2": striped8(np.stack([np.random.permutation(S) for _ in range(8)])),
        "cand": striped(np.random.permutation(T)[:C]),
        "n3": striped8(np.stack([np.random.permutation(S) for _ in range(8)])),
        "n4": striped8(np.stack([np.random.permutation(S) for _ in range(8)])),
    }


def reference(x_words, x_scales, d_words, d_scales, gs, offs, k1, n1, n2, cand, n3, n4):
    x_cand = unpack_weight(x_words, x_scales)[:, unstriped(cand)]
    d_k1 = unpack_weight(d_words, d_scales)[np.arange(K)[:, None], runs(k1, K)]
    xq = unpack_weight(x_words, x_scales)[:, unstriped(offs)]
    h = 0.0625 * (d_k1.T @ xq)
    st = np.maximum(h, h[np.arange(H)[:, None], runs(n1, H)])
    z = f64(gs) * (np.minimum(st, st[np.arange(H)[:, None], runs(n2, H)]))
    s = 0.0625 * ((x_cand.T @ mxq(z, 0, "e4m3")))
    return np.minimum(np.maximum(s, s[np.arange(C)[:, None], runs(n3, C)]), s[np.arange(C)[:, None], runs(n4, C)])

@@ -1,0 +1,212 @@
+from contextlib import ExitStack
+
+import concourse.mybir as mybir
+
+K, T, S, G = 512, 1024, 512, 2048
+FLOPS = 2 * 2 * 512 * 512 * 512
+
+F32 = mybir.dt.float32
+BF16 = mybir.dt.bfloat16
+I32 = mybir.dt.int32
+U32 = mybir.dt.uint32
+U16 = mybir.dt.uint16
+U8 = mybir.dt.uint8
+FP8X4 = mybir.dt.float8_e4m3fn_x4
+MAX = mybir.AluOpType.max
+MIN = mybir.AluOpType.min
+COPY = mybir.ActivationFunctionType.Copy
+
+P = 128
+PACK = 4
+HALF = S // 2
+
+
+def tile_picked_pqchopmnminmx_none_p_kernel(
+    tc, x_words, x_scales, d_words, d_scales, gs, offs, k1, n1, n2, cand, n3, n4, out
+):
+    nc = tc.nc
+    with ExitStack() as ctx:
+        keep = ctx.enter_context(tc.tile_pool(name="keep", bufs=1))
+        ring = ctx.enter_context(tc.tile_pool(name="ring", bufs=2))
+        psum = ctx.enter_context(tc.psum_pool(name="psum", bufs=1))
+
+        def new_list(name):
+            return keep.tile([P, S // 16], U16, name=name)
+
+        def gather(dst, table, offsets):
+            nc.vector.tensor_copy(dst, table[:].indirect(offsets))
+
+        def dealt(ap):
+            return ap.rearrange("p (m t) -> p t m", t=PACK)
+
+        def by_tile(ap):
+            return ap.rearrange("p (t m) -> p t m", t=PACK)
+
+        k1_sb, offs_sb, cand_sb = new_list("k1_sb"), new_list("offs_sb"), new_list("cand_sb")
+        n1_sb, n2_sb, n3_sb, n4_sb = new_list("n1_sb"), new_list("n2_sb"), new_list("n3_sb"), new_list("n4_sb")
+
+        ds_table = keep.tile([P, G], U8, name="ds_table")
+        xs_table = keep.tile([P, T], U8, name="xs_table")
+        dw_table = keep.tile([P, G], U32, name="dw_table")
+        xw_table = keep.tile([P, T], U32, name="xw_table")
+        d_scale = keep.tile([P, S], U8, name="d_scale", align_bytes=64)
+        gs_sb = keep.tile([P, PACK], F32, name="gs_sb")
+
+        nc.gpsimd.memset(ds_table[:].bitcast(I32), 0)
+        nc.vector.memset(xs_table[:].bitcast(I32), 0)
+
+        nc.sync.dma_start(offs_sb[:], offs)
+        nc.sync.dma_start(xw_table[:].bitcast(I32), x_words[0].rearrange("p n t -> p (n t)").bitcast(I32))
+        nc.sync.dma_start(k1_sb[:], k1)
+        for e in range(2):
+            nc.sync.dma_start(ds_table[e:P:16, :].bitcast(I32), d_scales[0, e:16:2, :].bitcast(I32))
+        for i in range(4):
+            nc.sync.dma_start(xs_table[i:P:32, :].bitcast(I32), x_scales[0, i:16:4, :].bitcast(I32))
+        nc.sync.dma_start(dw_table[:].bitcast(I32), d_words[0].rearrange("p n t -> p (n t)").bitcast(I32))
+        nc.sync.dma_start(cand_sb[:], cand)
+        nc.sync.dma_start(n1_sb[:], n1)
+        nc.sync.dma_start(n2_sb[:], n2)
+        nc.sync.dma_start(gs_sb[:], gs.rearrange("(p t) o -> p (t o)", t=PACK))
+        nc.sync.dma_start(n3_sb[:], n3)
+        nc.sync.dma_start(n4_sb[:], n4)
+
+        q_scale = keep.tile([P, S], U8, name="q_scale", align_bytes=64)
+        q_words = keep.tile([P, S], U32, name="q_words", align_bytes=64)
+        ds_picked = keep.tile([P, S], U8, name="ds_picked")
+        gather(q_words[:], xw_table, offs_sb[:])
+        gather(ds_picked[:], ds_table, k1_sb[:])
+        gather(q_scale[:], xs_table, offs_sb[:])
+        nc.vector.tensor_copy(by_tile(d_scale[:]), dealt(ds_picked[:]))
+        for e in range(2):
+            nc.sync.dma_start(d_scale[2 + e : P : 32, :].bitcast(I32), d_scale[16 + e : P : 32, :].bitcast(I32))
+
+        dw_picked = keep.tile([P, S], U32, name="dw_picked", tag="after_dw")
+        d_words_sb = keep.tile([P, S], U32, name="d_words_sb", align_bytes=64)
+        gather(dw_picked[:], dw_table, k1_sb[:])
+        nc.vector.tensor_copy(by_tile(d_words_sb[:]), dealt(dw_picked[:]))
+
+        cs_picked = keep.tile([P, S], U8, name="cs_picked", tag="after_dw")
+        c_scale = keep.tile([P, S], U8, name="c_scale", align_bytes=64)
+        gather(cs_picked[:], xs_table, cand_sb[:])
+        nc.vector.tensor_copy(by_tile(c_scale[:]), dealt(cs_picked[:]))
+
+        rows = [keep.tile([P, 2 * S], F32, name=f"rows{t}") for t in range(PACK)]
+        st = [keep.tile([P, 2 * S], F32, name=f"st{u}") for u in range(2)]
+        for window in rows + st:
+            nc.vector.memset(window[:, S:], 0.0)
+
+        for t in range(PACK):
+            cols = slice(t * P, (t + 1) * P)
+            h_psum = psum.tile([P, S], F32, name=f"h_psum{t}")
+            nc.tensor.matmul_mx(
+                out=h_psum[:],
+                lhsT=d_words_sb[:, cols].bitcast(FP8X4),
+                lhsT_scale=d_scale[:, cols],
+                rhs=q_words[:].bitcast(FP8X4),
+                rhs_scale=q_scale[:],
+                start=True,
+                stop=True,
+            )
+            nc.scalar.activation(rows[t][:, :S], h_psum[:], COPY, scale=0.0625)
+
+        z = [keep.tile([P, HALF, PACK], BF16, name=f"z{u}", align_bytes=64) for u in range(2)]
+        h_n1, st_n2 = {}, {}
+
+        def fetch_h(t):
+            h_n1[t] = ring.tile([P, S], F32, name="h_n1")
+            gather(h_n1[t][:], rows[t], n1_sb[:])
+
+        def larger(t):
+            nc.vector.tensor_tensor(st[t % 2][:, :S], h_n1[t][:], rows[t][:, :S], MAX)
+
+        def fetch_st(t):
+            st_n2[t] = ring.tile([P, S], F32, name="st_n2")
+            gather(st_n2[t][:], st[t % 2], n2_sb[:])
+
+        def weigh(t, u, smaller_half):
+            nc.scalar.activation(z[u][:, :, t], smaller_half, COPY, scale=gs_sb[:, t : t + 1])
+
+        def smaller(t):
+            m = ring.tile([P, S], F32, name="m")
+            nc.vector.tensor_tensor(m[:], st_n2[t][:], st[t % 2][:, :S], MIN)
+            for u in range(2):
+                weigh(t, u, m[:, u * HALF : (u + 1) * HALF])
+
+        fetch_h(0)
+        fetch_h(1)
+        larger(0)
+        fetch_h(2)
+        larger(1)
+        fetch_st(0)
+        fetch_h(3)
+        smaller(0)
+        fetch_st(1)
+        larger(2)
+        smaller(1)
+        fetch_st(2)
+        larger(3)
+        smaller(2)
+        last = PACK - 1
+        halves = [keep.tile([P, HALF], F32, name=f"st_n2_last{u}", tag=f"last{u}") for u in range(2)]
+        for u in range(2):
+            gather(halves[u][:], st[last % 2], n2_sb[:, 16 * u : 16 * (u + 1)])
+        for u in range(2):
+            m_half = keep.tile([P, HALF], F32, name=f"m_last{u}")
+            nc.vector.tensor_tensor(m_half[:], halves[u][:], st[last % 2][:, u * HALF : (u + 1) * HALF], MIN)
+            weigh(last, u, m_half[:])
+
+        cw_picked = keep.tile([P, S], U32, name="cw_picked", tag="last1")
+        c_words = keep.tile([P, S], U32, name="c_words", align_bytes=64)
+        gather(cw_picked[:], xw_table, cand_sb[:])
+        nc.vector.tensor_copy(by_tile(c_words[:]), dealt(cw_picked[:]))
+
+        s_psum = [psum.tile([P, S], F32, name=f"s_psum{t}") for t in range(PACK)]
+        for u in range(2):
+            z_words = keep.tile([P, HALF], U32, name=f"z_words{u}", align_bytes=64)
+            z_scale = keep.tile([P, HALF], U8, name=f"z_scale{u}", align_bytes=64)
+            nc.vector.quantize_mx(
+                out=z_words[:].bitcast(FP8X4),
+                scales=z_scale[:],
+                in_=z[u][:].rearrange("p j t -> p (j t)"),
+            )
+            for t in range(PACK):
+                cols = slice(t * P, (t + 1) * P)
+                nc.tensor.matmul_mx(
+                    out=s_psum[t][:, u * HALF : (u + 1) * HALF],
+                    lhsT=c_words[:, cols].bitcast(FP8X4),
+                    lhsT_scale=c_scale[:, cols],
+                    rhs=z_words[:].bitcast(FP8X4),
+                    rhs_scale=z_scale[:],
+                    start=True,
+                    stop=True,
+                )
+        for t in range(PACK):
+            nc.scalar.activation(rows[t][:, :S], s_psum[t][:], COPY, scale=0.0625)
+
+        out_rows = out.rearrange("(p t) n -> t p n", t=PACK)
+        s_n3, s_n4, upper = {}, {}, {}
+
+        def fetch_n3(t):
+            s_n3[t] = ring.tile([P, S], F32, name="s_n3")
+            gather(s_n3[t][:], rows[t], n3_sb[:])
+
+        def fetch_n4(t):
+            s_n4[t] = ring.tile([P, S], F32, name="s_n4")
+            gather(s_n4[t][:], rows[t], n4_sb[:])
+
+        def raise_(t):
+            upper[t] = ring.tile([P, S], F32, name="upper")
+            nc.vector.tensor_tensor(upper[t][:], s_n3[t][:], rows[t][:, :S], MAX)
+
+        def finish(t):
+            result = keep.tile([P, S], F32, name=f"result{t}")
+            nc.vector.tensor_tensor(result[:], upper[t][:], s_n4[t][:], MIN)
+            nc.sync.dma_start(out_rows[t], result[:])
+
+        for t in range(PACK):
+            fetch_n3(t)
+            if t > 0:
+                finish(t - 1)
+            fetch_n4(t)
+            raise_(t)
+        finish(last)

@@ -52,62 +52,77 @@ def tile_picked_pqchopmnminmx_none_p_kernel(
         d_scale = keep.tile([P, S], U8, name="d_scale", align_bytes=64)
         gs_sb = keep.tile([P, PACK], F32, name="gs_sb")
 
-        nc.gpsimd.memset(ds_table[:].bitcast(I32), 0)
-        nc.vector.memset(xs_table[:].bitcast(I32), 0)
-
-        nc.sync.dma_start(offs_sb[:], offs)
-        nc.sync.dma_start(xw_table[:].bitcast(I32), x_words[0].rearrange("p n t -> p (n t)").bitcast(I32))
         nc.sync.dma_start(k1_sb[:], k1)
-        for e in range(2):
-            nc.sync.dma_start(ds_table[e:P:16, :].bitcast(I32), d_scales[0, e:16:2, :].bitcast(I32))
-        for i in range(4):
-            nc.sync.dma_start(xs_table[i:P:32, :].bitcast(I32), x_scales[0, i:16:4, :].bitcast(I32))
-        nc.sync.dma_start(dw_table[:].bitcast(I32), d_words[0].rearrange("p n t -> p (n t)").bitcast(I32))
+        nc.sync.dma_start(
+            ds_table[:].bitcast(I32), d_scales[0].bitcast(I32).unsqueeze(1).broadcast_to([16, 8, G // 4])
+        )
+        nc.sync.dma_start(offs_sb[:], offs)
+        for q in range(4):
+            nc.sync.dma_start(
+                xs_table[32 * q : 32 * (q + 1), :].bitcast(I32),
+                x_scales[0, 4 * q : 4 * (q + 1), :].bitcast(I32).unsqueeze(0).broadcast_to([8, 4, T // 4]),
+            )
+        nc.sync.dma_start(xw_table[:].bitcast(I32), x_words[0].rearrange("p n t -> p (n t)").bitcast(I32))
         nc.sync.dma_start(cand_sb[:], cand)
         nc.sync.dma_start(n1_sb[:], n1)
+        nc.sync.dma_start(dw_table[:].bitcast(I32), d_words[0].rearrange("p n t -> p (n t)").bitcast(I32))
         nc.sync.dma_start(n2_sb[:], n2)
         nc.sync.dma_start(gs_sb[:], gs.rearrange("(p t) o -> p (t o)", t=PACK))
         nc.sync.dma_start(n3_sb[:], n3)
         nc.sync.dma_start(n4_sb[:], n4)
 
         q_scale = keep.tile([P, S], U8, name="q_scale", align_bytes=64)
-        q_words = keep.tile([P, S], U32, name="q_words", align_bytes=64)
         ds_picked = keep.tile([P, S], U8, name="ds_picked")
-        gather(q_words[:], xw_table, offs_sb[:])
         gather(ds_picked[:], ds_table, k1_sb[:])
-        gather(q_scale[:], xs_table, offs_sb[:])
         nc.vector.tensor_copy(by_tile(d_scale[:]), dealt(ds_picked[:]))
-        for e in range(2):
-            nc.sync.dma_start(d_scale[2 + e : P : 32, :].bitcast(I32), d_scale[16 + e : P : 32, :].bitcast(I32))
+        for i in range(1, 4):
+            nc.sync.dma_start(d_scale[i:P:32, :].bitcast(I32), d_scale[8 * i : P : 32, :].bitcast(I32))
+        gather(q_scale[:], xs_table, offs_sb[:])
+        q_words = keep.tile([P, S], U32, name="q_words", align_bytes=64)
+        gather(q_words[:], xw_table, offs_sb[:])
 
         dw_picked = keep.tile([P, S], U32, name="dw_picked", tag="after_dw")
         d_words_sb = keep.tile([P, S], U32, name="d_words_sb", align_bytes=64)
         gather(dw_picked[:], dw_table, k1_sb[:])
-        nc.vector.tensor_copy(by_tile(d_words_sb[:]), dealt(dw_picked[:]))
+        nc.vector.tensor_copy(by_tile(d_words_sb[:])[:, 0, :], dealt(dw_picked[:])[:, 0, :])
+        nc.vector.tensor_copy(by_tile(d_words_sb[:])[:, 1:, :], dealt(dw_picked[:])[:, 1:, :])
 
         cs_picked = keep.tile([P, S], U8, name="cs_picked", tag="after_dw")
         c_scale = keep.tile([P, S], U8, name="c_scale", align_bytes=64)
         gather(cs_picked[:], xs_table, cand_sb[:])
-        nc.vector.tensor_copy(by_tile(c_scale[:]), dealt(cs_picked[:]))
+        nc.vector.tensor_copy(
+            c_scale[:].bitcast(I32).rearrange("p (t r w) -> p t r w", t=PACK, r=8),
+            cs_picked[:].bitcast(I32).rearrange("p (r t w) -> p t r w", t=PACK, r=8),
+        )
 
         rows = [keep.tile([P, 2 * S], F32, name=f"rows{t}") for t in range(PACK)]
         st = [keep.tile([P, 2 * S], F32, name=f"st{u}") for u in range(2)]
-        for window in rows + st:
-            nc.vector.memset(window[:, S:], 0.0)
+        nc.vector.memset(rows[0][:, S:], 0.0)
+        for window in rows[1:] + st:
+            nc.scalar.copy(window[:, S:], rows[0][:, S:])
 
-        for t in range(PACK):
-            cols = slice(t * P, (t + 1) * P)
-            h_psum = psum.tile([P, S], F32, name=f"h_psum{t}")
+        def product(t, cols, bank, words, scale, moving_words, moving_scale):
+            width = cols.stop - cols.start
+            acc = psum.tile([P, width], F32, name="acc", tag=f"bank{bank}")
+            stationary = slice(t * P, (t + 1) * P)
             nc.tensor.matmul_mx(
-                out=h_psum[:],
-                lhsT=d_words_sb[:, cols].bitcast(FP8X4),
-                lhsT_scale=d_scale[:, cols],
-                rhs=q_words[:].bitcast(FP8X4),
-                rhs_scale=q_scale[:],
+                out=acc[:],
+                lhsT=words[:, stationary].bitcast(FP8X4),
+                lhsT_scale=scale[:, stationary],
+                rhs=moving_words[:, cols].bitcast(FP8X4),
+                rhs_scale=moving_scale[:, cols],
                 start=True,
                 stop=True,
             )
-            nc.scalar.activation(rows[t][:, :S], h_psum[:], COPY, scale=0.0625)
+            nc.scalar.activation(rows[t][:, cols], acc[:], COPY, scale=0.0625)
+
+        def products(*operands):
+            for u in range(2):
+                product(0, slice(u * HALF, (u + 1) * HALF), u, *operands)
+            for t in range(1, PACK):
+                product(t, slice(0, S), 1 + t, *operands)
+
+        products(d_words_sb, d_scale, q_words, q_scale)
 
         z = [keep.tile([P, HALF, PACK], BF16, name=f"z{u}", align_bytes=64) for u in range(2)]
         h_n1, st_n2 = {}, {}
@@ -147,7 +162,7 @@ def tile_picked_pqchopmnminmx_none_p_kernel(
         larger(3)
         smaller(2)
         last = PACK - 1
-        halves = [keep.tile([P, HALF], F32, name=f"st_n2_last{u}", tag=f"last{u}") for u in range(2)]
+        halves = [keep.tile([P, HALF], F32, name=f"st_n2_last{u}", tag=f"last{u}", align_bytes=64) for u in range(2)]
         for u in range(2):
             gather(halves[u][:], st[last % 2], n2_sb[:, 16 * u : 16 * (u + 1)])
         for u in range(2):
@@ -155,35 +170,21 @@ def tile_picked_pqchopmnminmx_none_p_kernel(
             nc.vector.tensor_tensor(m_half[:], halves[u][:], st[last % 2][:, u * HALF : (u + 1) * HALF], MIN)
             weigh(last, u, m_half[:])
 
-        cw_picked = keep.tile([P, S], U32, name="cw_picked", tag="last1")
-        c_words = keep.tile([P, S], U32, name="c_words", align_bytes=64)
-        gather(cw_picked[:], xw_table, cand_sb[:])
-        nc.vector.tensor_copy(by_tile(c_words[:]), dealt(cw_picked[:]))
+        c_words = keep.tile([P, S], U32, name="c_words", tag="last1", align_bytes=64)
+        gather(c_words[:].rearrange("p (t r u) -> p r t u", t=PACK, r=8), xw_table, cand_sb[:])
 
-        s_psum = [psum.tile([P, S], F32, name=f"s_psum{t}") for t in range(PACK)]
+        z_words = keep.tile([P, S], U32, name="z_words", align_bytes=64)
+        z_scale = keep.tile([P, S], U8, name="z_scale", align_bytes=64)
         for u in range(2):
-            z_words = keep.tile([P, HALF], U32, name=f"z_words{u}", align_bytes=64)
-            z_scale = keep.tile([P, HALF], U8, name=f"z_scale{u}", align_bytes=64)
+            cols = slice(u * HALF, (u + 1) * HALF)
             nc.vector.quantize_mx(
-                out=z_words[:].bitcast(FP8X4),
-                scales=z_scale[:],
+                out=z_words[:, cols].bitcast(FP8X4),
+                scales=z_scale[:, cols],
                 in_=z[u][:].rearrange("p j t -> p (j t)"),
             )
-            for t in range(PACK):
-                cols = slice(t * P, (t + 1) * P)
-                nc.tensor.matmul_mx(
-                    out=s_psum[t][:, u * HALF : (u + 1) * HALF],
-                    lhsT=c_words[:, cols].bitcast(FP8X4),
-                    lhsT_scale=c_scale[:, cols],
-                    rhs=z_words[:].bitcast(FP8X4),
-                    rhs_scale=z_scale[:],
-                    start=True,
-                    stop=True,
-                )
-        for t in range(PACK):
-            nc.scalar.activation(rows[t][:, :S], s_psum[t][:], COPY, scale=0.0625)
+        products(c_words, c_scale, z_words, z_scale)
 
-        out_rows = out.rearrange("(p t) n -> t p n", t=PACK)
+        out_rows = out.rearrange("(r t u) n -> t r u n", t=PACK, r=8)
         s_n3, s_n4, upper = {}, {}, {}
 
         def fetch_n3(t):
@@ -203,10 +204,20 @@ def tile_picked_pqchopmnminmx_none_p_kernel(
             nc.vector.tensor_tensor(result[:], upper[t][:], s_n4[t][:], MIN)
             nc.sync.dma_start(out_rows[t], result[:])
 
-        for t in range(PACK):
+        for t in range(last):
             fetch_n3(t)
             if t > 0:
                 finish(t - 1)
             fetch_n4(t)
             raise_(t)
-        finish(last)
+        fetch_n3(last)
+        finish(last - 1)
+        raise_(last)
+        s_n4_half = [keep.tile([P, HALF], F32, name=f"s_n4_half{u}") for u in range(2)]
+        for u in range(2):
+            gather(s_n4_half[u][:], rows[last], n4_sb[:, 16 * u : 16 * (u + 1)])
+        for u, queue in enumerate((nc.scalar, nc.sync)):
+            cols = slice(u * HALF, (u + 1) * HALF)
+            result_half = keep.tile([P, HALF], F32, name=f"result_half{u}")
+            nc.vector.tensor_tensor(result_half[:], upper[last][:, cols], s_n4_half[u][:], MIN)
+            queue.dma_start(out_rows[last][:, :, cols], result_half[:])

@@ -52,21 +52,18 @@ def tile_picked_pqchopmnminmx_none_p_kernel(
         d_scale = keep.tile([P, S], U8, name="d_scale", align_bytes=64)
         gs_sb = keep.tile([P, PACK], F32, name="gs_sb")
 
+        nc.vector.memset(ds_table[:].bitcast(I32), 0)
+        nc.gpsimd.memset(xs_table[:].bitcast(I32), 0)
         nc.sync.dma_start(k1_sb[:], k1)
-        nc.sync.dma_start(
-            ds_table[:].bitcast(I32), d_scales[0].bitcast(I32).unsqueeze(1).broadcast_to([16, 8, G // 4])
-        )
         nc.sync.dma_start(offs_sb[:], offs)
-        for q in range(4):
-            nc.sync.dma_start(
-                xs_table[32 * q : 32 * (q + 1), :].bitcast(I32),
-                x_scales[0, 4 * q : 4 * (q + 1), :].bitcast(I32).unsqueeze(0).broadcast_to([8, 4, T // 4]),
-            )
-        nc.sync.dma_start(xw_table[:].bitcast(I32), x_words[0].rearrange("p n t -> p (n t)").bitcast(I32))
         nc.sync.dma_start(cand_sb[:], cand)
         nc.sync.dma_start(n1_sb[:], n1)
-        nc.sync.dma_start(dw_table[:].bitcast(I32), d_words[0].rearrange("p n t -> p (n t)").bitcast(I32))
         nc.sync.dma_start(n2_sb[:], n2)
+        nc.sync.dma_start(ds_table[0:P:8, :].bitcast(I32), d_scales[0].bitcast(I32))
+        nc.sync.dma_start(xw_table[:].bitcast(I32), x_words[0].rearrange("p n t -> p (n t)").bitcast(I32))
+        for i in range(4):
+            nc.sync.dma_start(xs_table[i:P:32, :].bitcast(I32), x_scales[0, i:16:4, :].bitcast(I32))
+        nc.sync.dma_start(dw_table[:].bitcast(I32), d_words[0].rearrange("p n t -> p (n t)").bitcast(I32))
         nc.sync.dma_start(gs_sb[:], gs.rearrange("(p t) o -> p (t o)", t=PACK))
         nc.sync.dma_start(n3_sb[:], n3)
         nc.sync.dma_start(n4_sb[:], n4)
@@ -91,8 +88,8 @@ def tile_picked_pqchopmnminmx_none_p_kernel(
         c_scale = keep.tile([P, S], U8, name="c_scale", align_bytes=64)
         gather(cs_picked[:], xs_table, cand_sb[:])
         nc.vector.tensor_copy(
-            c_scale[:].bitcast(I32).rearrange("p (t r w) -> p t r w", t=PACK, r=8),
-            cs_picked[:].bitcast(I32).rearrange("p (r t w) -> p t r w", t=PACK, r=8),
+            c_scale[:].bitcast(I32).rearrange("p (t g w) -> p t g w", t=PACK, g=16),
+            cs_picked[:].bitcast(I32).rearrange("p (g t w) -> p t g w", t=PACK, g=16),
         )
 
         rows = [keep.tile([P, 2 * S], F32, name=f"rows{t}") for t in range(PACK)]
@@ -171,7 +168,7 @@ def tile_picked_pqchopmnminmx_none_p_kernel(
             weigh(last, u, m_half[:])
 
         c_words = keep.tile([P, S], U32, name="c_words", tag="last1", align_bytes=64)
-        gather(c_words[:].rearrange("p (t r u) -> p r t u", t=PACK, r=8), xw_table, cand_sb[:])
+        gather(c_words[:].rearrange("p (t g v) -> p g t v", t=PACK, g=16), xw_table, cand_sb[:])
 
         z_words = keep.tile([P, S], U32, name="z_words", align_bytes=64)
         z_scale = keep.tile([P, S], U8, name="z_scale", align_bytes=64)
@@ -184,7 +181,7 @@ def tile_picked_pqchopmnminmx_none_p_kernel(
             )
         products(c_words, c_scale, z_words, z_scale)
 
-        out_rows = out.rearrange("(r t u) n -> t r u n", t=PACK, r=8)
+        out_rows = out.rearrange("(g t v) n -> t g v n", t=PACK, g=16)
         s_n3, s_n4, upper = {}, {}, {}
 
         def fetch_n3(t):

from contextlib import ExitStack

import concourse.mybir as mybir

K, T, S, G = 512, 1024, 512, 2048
FLOPS = 2 * 2 * 512 * 512 * 512

F32 = mybir.dt.float32
BF16 = mybir.dt.bfloat16
I32 = mybir.dt.int32
U32 = mybir.dt.uint32
U16 = mybir.dt.uint16
U8 = mybir.dt.uint8
FP8X4 = mybir.dt.float8_e4m3fn_x4
MAX = mybir.AluOpType.max
MIN = mybir.AluOpType.min
COPY = mybir.ActivationFunctionType.Copy

P = 128
PACK = 4
HALF = S // 2


def tile_picked_pqchopmnminmx_none_p_kernel(
    tc, x_words, x_scales, d_words, d_scales, gs, offs, k1, n1, n2, cand, n3, n4, out
):
    nc = tc.nc
    with ExitStack() as ctx:
        keep = ctx.enter_context(tc.tile_pool(name="keep", bufs=1))
        ring = ctx.enter_context(tc.tile_pool(name="ring", bufs=2))
        psum = ctx.enter_context(tc.psum_pool(name="psum", bufs=1))

        def new_list(name):
            return keep.tile([P, S // 16], U16, name=name)

        def gather(dst, table, offsets):
            nc.vector.tensor_copy(dst, table[:].indirect(offsets))

        def dealt(ap):
            return ap.rearrange("p (m t) -> p t m", t=PACK)

        def by_tile(ap):
            return ap.rearrange("p (t m) -> p t m", t=PACK)

        k1_sb, offs_sb, cand_sb = new_list("k1_sb"), new_list("offs_sb"), new_list("cand_sb")
        n1_sb, n2_sb, n3_sb, n4_sb = new_list("n1_sb"), new_list("n2_sb"), new_list("n3_sb"), new_list("n4_sb")

        ds_table = keep.tile([P, G], U8, name="ds_table")
        xs_table = keep.tile([P, T], U8, name="xs_table")
        dw_table = keep.tile([P, G], U32, name="dw_table")
        xw_table = keep.tile([P, T], U32, name="xw_table")
        d_scale = keep.tile([P, S], U8, name="d_scale", align_bytes=64)
        gs_sb = keep.tile([P, PACK], F32, name="gs_sb")

        nc.vector.memset(ds_table[:].bitcast(I32), 0)
        nc.gpsimd.memset(xs_table[:].bitcast(I32), 0)
        nc.sync.dma_start(k1_sb[:], k1)
        nc.sync.dma_start(offs_sb[:], offs)
        nc.sync.dma_start(cand_sb[:], cand)
        nc.sync.dma_start(n1_sb[:], n1)
        nc.sync.dma_start(n2_sb[:], n2)
        nc.sync.dma_start(ds_table[0:P:8, :].bitcast(I32), d_scales[0].bitcast(I32))
        nc.sync.dma_start(xw_table[:].bitcast(I32), x_words[0].rearrange("p n t -> p (n t)").bitcast(I32))
        for i in range(4):
            nc.sync.dma_start(xs_table[i:P:32, :].bitcast(I32), x_scales[0, i:16:4, :].bitcast(I32))
        nc.sync.dma_start(dw_table[:].bitcast(I32), d_words[0].rearrange("p n t -> p (n t)").bitcast(I32))
        nc.sync.dma_start(gs_sb[:], gs.rearrange("(p t) o -> p (t o)", t=PACK))
        nc.sync.dma_start(n3_sb[:], n3)
        nc.sync.dma_start(n4_sb[:], n4)

        q_scale = keep.tile([P, S], U8, name="q_scale", align_bytes=64)
        ds_picked = keep.tile([P, S], U8, name="ds_picked")
        gather(ds_picked[:], ds_table, k1_sb[:])
        nc.vector.tensor_copy(by_tile(d_scale[:]), dealt(ds_picked[:]))
        for i in range(1, 4):
            nc.sync.dma_start(d_scale[i:P:32, :].bitcast(I32), d_scale[8 * i : P : 32, :].bitcast(I32))
        gather(q_scale[:], xs_table, offs_sb[:])
        q_words = keep.tile([P, S], U32, name="q_words", align_bytes=64)
        gather(q_words[:], xw_table, offs_sb[:])

        dw_picked = keep.tile([P, S], U32, name="dw_picked", tag="after_dw")
        d_words_sb = keep.tile([P, S], U32, name="d_words_sb", align_bytes=64)
        gather(dw_picked[:], dw_table, k1_sb[:])
        nc.vector.tensor_copy(by_tile(d_words_sb[:])[:, 0, :], dealt(dw_picked[:])[:, 0, :])
        nc.vector.tensor_copy(by_tile(d_words_sb[:])[:, 1:, :], dealt(dw_picked[:])[:, 1:, :])

        cs_picked = keep.tile([P, S], U8, name="cs_picked", tag="after_dw")
        c_scale = keep.tile([P, S], U8, name="c_scale", align_bytes=64)
        gather(cs_picked[:], xs_table, cand_sb[:])
        nc.vector.tensor_copy(
            c_scale[:].bitcast(I32).rearrange("p (t g w) -> p t g w", t=PACK, g=16),
            cs_picked[:].bitcast(I32).rearrange("p (g t w) -> p t g w", t=PACK, g=16),
        )

        rows = [keep.tile([P, 2 * S], F32, name=f"rows{t}") for t in range(PACK)]
        st = [keep.tile([P, 2 * S], F32, name=f"st{u}") for u in range(2)]
        nc.vector.memset(rows[0][:, S:], 0.0)
        for window in rows[1:] + st:
            nc.scalar.copy(window[:, S:], rows[0][:, S:])

        def product(t, cols, bank, words, scale, moving_words, moving_scale):
            width = cols.stop - cols.start
            acc = psum.tile([P, width], F32, name="acc", tag=f"bank{bank}")
            stationary = slice(t * P, (t + 1) * P)
            nc.tensor.matmul_mx(
                out=acc[:],
                lhsT=words[:, stationary].bitcast(FP8X4),
                lhsT_scale=scale[:, stationary],
                rhs=moving_words[:, cols].bitcast(FP8X4),
                rhs_scale=moving_scale[:, cols],
                start=True,
                stop=True,
            )
            nc.scalar.activation(rows[t][:, cols], acc[:], COPY, scale=0.0625)

        def products(*operands):
            for u in range(2):
                product(0, slice(u * HALF, (u + 1) * HALF), u, *operands)
            for t in range(1, PACK):
                product(t, slice(0, S), 1 + t, *operands)

        products(d_words_sb, d_scale, q_words, q_scale)

        z = [keep.tile([P, HALF, PACK], BF16, name=f"z{u}", align_bytes=64) for u in range(2)]
        h_n1, st_n2 = {}, {}

        def fetch_h(t):
            h_n1[t] = ring.tile([P, S], F32, name="h_n1")
            gather(h_n1[t][:], rows[t], n1_sb[:])

        def larger(t):
            nc.vector.tensor_tensor(st[t % 2][:, :S], h_n1[t][:], rows[t][:, :S], MAX)

        def fetch_st(t):
            st_n2[t] = ring.tile([P, S], F32, name="st_n2")
            gather(st_n2[t][:], st[t % 2], n2_sb[:])

        def weigh(t, u, smaller_half):
            nc.scalar.activation(z[u][:, :, t], smaller_half, COPY, scale=gs_sb[:, t : t + 1])

        def smaller(t):
            m = ring.tile([P, S], F32, name="m")
            nc.vector.tensor_tensor(m[:], st_n2[t][:], st[t % 2][:, :S], MIN)
            for u in range(2):
                weigh(t, u, m[:, u * HALF : (u + 1) * HALF])

        fetch_h(0)
        fetch_h(1)
        larger(0)
        fetch_h(2)
        larger(1)
        fetch_st(0)
        fetch_h(3)
        smaller(0)
        fetch_st(1)
        larger(2)
        smaller(1)
        fetch_st(2)
        larger(3)
        smaller(2)
        last = PACK - 1
        halves = [keep.tile([P, HALF], F32, name=f"st_n2_last{u}", tag=f"last{u}", align_bytes=64) for u in range(2)]
        for u in range(2):
            gather(halves[u][:], st[last % 2], n2_sb[:, 16 * u : 16 * (u + 1)])
        for u in range(2):
            m_half = keep.tile([P, HALF], F32, name=f"m_last{u}")
            nc.vector.tensor_tensor(m_half[:], halves[u][:], st[last % 2][:, u * HALF : (u + 1) * HALF], MIN)
            weigh(last, u, m_half[:])

        c_words = keep.tile([P, S], U32, name="c_words", tag="last1", align_bytes=64)
        gather(c_words[:].rearrange("p (t g v) -> p g t v", t=PACK, g=16), xw_table, cand_sb[:])

        z_words = keep.tile([P, S], U32, name="z_words", align_bytes=64)
        z_scale = keep.tile([P, S], U8, name="z_scale", align_bytes=64)
        for u in range(2):
            cols = slice(u * HALF, (u + 1) * HALF)
            nc.vector.quantize_mx(
                out=z_words[:, cols].bitcast(FP8X4),
                scales=z_scale[:, cols],
                in_=z[u][:].rearrange("p j t -> p (j t)"),
            )
        products(c_words, c_scale, z_words, z_scale)

        out_rows = out.rearrange("(g t v) n -> t g v n", t=PACK, g=16)
        s_n3, s_n4, upper = {}, {}, {}

        def fetch_n3(t):
            s_n3[t] = ring.tile([P, S], F32, name="s_n3")
            gather(s_n3[t][:], rows[t], n3_sb[:])

        def fetch_n4(t):
            s_n4[t] = ring.tile([P, S], F32, name="s_n4")
            gather(s_n4[t][:], rows[t], n4_sb[:])

        def raise_(t):
            upper[t] = ring.tile([P, S], F32, name="upper")
            nc.vector.tensor_tensor(upper[t][:], s_n3[t][:], rows[t][:, :S], MAX)

        def finish(t):
            result = keep.tile([P, S], F32, name=f"result{t}")
            nc.vector.tensor_tensor(result[:], upper[t][:], s_n4[t][:], MIN)
            nc.sync.dma_start(out_rows[t], result[:])

        for t in range(last):
            fetch_n3(t)
            if t > 0:
                finish(t - 1)
            fetch_n4(t)
            raise_(t)
        fetch_n3(last)
        finish(last - 1)
        raise_(last)
        s_n4_half = [keep.tile([P, HALF], F32, name=f"s_n4_half{u}") for u in range(2)]
        for u in range(2):
            gather(s_n4_half[u][:], rows[last], n4_sb[:, 16 * u : 16 * (u + 1)])
        for u, queue in enumerate((nc.scalar, nc.sync)):
            cols = slice(u * HALF, (u + 1) * HALF)
            result_half = keep.tile([P, HALF], F32, name=f"result_half{u}")
            nc.vector.tensor_tensor(result_half[:], upper[last][:, cols], s_n4_half[u][:], MIN)
            queue.dma_start(out_rows[last][:, :, cols], result_half[:])
